import numpy as np
import ml_dtypes


def mxq(x, axis, fmt="e4m3"):
    dtype, down = {"e4m3": (ml_dtypes.float8_e4m3fn, 7), "e5m2": (ml_dtypes.float8_e5m2, 14)}[fmt]
    v = np.moveaxis(np.asarray(x, np.float32).astype(ml_dtypes.bfloat16).astype(np.float64), axis, -1)
    blocks = v.reshape(v.shape[:-1] + (-1, 32))
    amax = np.abs(blocks).max(-1, keepdims=True)
    byte = np.maximum(np.where(amax > 0, np.frexp(amax)[1] - 1 + 127, 0) - down, 1)
    scale = np.exp2(byte - 127.0)
    codes = (blocks / scale).astype(np.float32).astype(dtype).astype(np.float64)
    return np.moveaxis((codes * scale).reshape(v.shape), -1, axis)


WIDE = False


def mx_kscale(k):
    if not WIDE:
        return np.ones(k)
    levels = np.array([10, -10, 5, -5, 0])
    if k % 512:
        return np.exp2(np.random.permutation(np.resize(levels, k // 32))).repeat(32)
    a = np.empty((k // 512, 16))
    for p in range(k // 512):
        a[p, :8] = np.random.permutation(np.resize(levels, 8))
        for g in range(8):
            far = levels[np.abs(levels - a[p, g]) >= 10]
            a[p, g + 8] = far[np.random.randint(len(far))]
    return np.exp2(a.ravel()).repeat(32)


BF16 = ml_dtypes.bfloat16


def bf(x):
    return np.asarray(x, np.float32).astype(BF16)


def f64(x):
    return np.asarray(x).astype(np.float64)


E2M1 = np.array([0.0, 0.5, 1.0, 1.5, 2.0, 3.0, 4.0, 6.0, -0.0, -0.5, -1.0, -1.5, -2.0, -3.0, -4.0, -6.0])


def pack_weight(w, fmt):
    k, n = w.shape
    w = f64(bf(w)).reshape(k // 32, 32, n)
    amax = np.abs(w).max(1)
    if fmt == "e4m3":
        byte = np.frexp(amax)[1] - 1 + 127 - 7
    else:
        mant, ex = np.frexp(amax / 6.0)
        byte = np.where(mant > 0.5, ex, ex - 1) + 127
    byte = np.clip(np.where(amax > 0, byte, 1), 1, 254)
    scaled = (w * np.exp2(127.0 - byte)[:, None, :]).reshape(k, n).astype(np.float32)
    by_word = np.ascontiguousarray(scaled.reshape(k // 512, 128, 4, n).transpose(0, 1, 3, 2))
    if fmt == "e4m3":
        words = by_word.astype(ml_dtypes.float8_e4m3fn).view(np.uint8)
    else:
        c = by_word.astype(ml_dtypes.float4_e2m1fn).view(np.uint8) & 0xF
        words = c[..., 0::2] | (c[..., 1::2] << 4)
    return np.ascontiguousarray(words), np.ascontiguousarray(byte.astype(np.uint8).reshape(k // 512, 16, n))


def unpack_weight(words, scales, fmt):
    g, p, n, _ = words.shape
    if fmt == "e4m3":
        vals = np.ascontiguousarray(words).view(ml_dtypes.float8_e4m3fn).astype(np.float64)
    else:
        nib = np.empty((g, p, n, 4), np.uint8)
        nib[..., 0::2] = words & 0xF
        nib[..., 1::2] = words >> 4
        vals = E2M1[nib]
    vals = vals * np.repeat(np.exp2(scales.astype(np.float64) - 127.0), 8, axis=1)[..., None]
    return vals.transpose(0, 1, 3, 2).reshape(g * 512, n)
def pack4(w):
    words, scales = pack_weight(w, "e2m1")
    return words.reshape(words.shape[0], 128, -1), scales


def unpack4(words, scales):
    return unpack_weight(words.reshape(words.shape[0], 128, -1, 2), scales, "e2m1")


E, L, A, F = 2048, 1024, 1536, 512


def draw0():
    s = mx_kscale(L)
    u = mx_kscale(E)
    d = np.random.standard_normal((E, L)) * s * u[:, None]
    basis = np.random.standard_normal((L, A)) / np.sqrt(L) / s[:, None]
    r = 1.5 * np.random.standard_normal(E)
    frozen = np.random.standard_normal((E, F)) / np.sqrt(E) / u[:, None]
    ja_words, ja_scales = pack4(frozen)
    return {"d": bf(d),
            "basis": bf(basis),
            "r": bf(r),
            "ja_words": ja_words,
            "ja_scales": ja_scales}


def core(d, basis, r, ja_words, ja_scales):
    jb = mxq(f64(d), 1, "e4m3") @ mxq(f64(basis), 0, "e4m3")
    rr = f64(r)[:, None]
    wj = jb / (1.0 + rr * rr)
    ja = unpack4(ja_words, ja_scales)
    h = ja.T @ mxq(wj, 0, "e4m3")
    return h


def e4m3fn_bytes(y):
    return np.clip(np.asarray(y, np.float64), -448.0, 448.0).astype(np.float32).astype(ml_dtypes.float8_e4m3fn).view(np.uint8)


def e4m3fn_values(b):
    return np.asarray(b, np.uint8).view(ml_dtypes.float8_e4m3fn).astype(np.float64)


def setup_inputs():
    d = draw0()
    x0 = np.asarray(d['basis']).astype(np.float64)
    s = (np.max(np.abs(x0), axis=(1,), keepdims=True) / 448.0).astype(np.float32)
    out = {}
    for k, v in d.items():
        if k == 'basis':
            out['basis_bytes'] = e4m3fn_bytes(x0 / s.astype(np.float64))
            out['basis_scale'] = s
        else:
            out[k] = v
    return out


def reference(d, basis_bytes, basis_scale, r, ja_words, ja_scales):
    return core(d, e4m3fn_values(basis_bytes) * basis_scale.astype(np.float64), r, ja_words, ja_scales)

@@ -1,0 +1,355 @@
+from contextlib import ExitStack
+
+import concourse.mybir as mybir
+from concourse.masks import make_identity
+
+E, L, A, F = 2048, 1024, 1536, 512
+FLOPS = 2 * E * L * A + 2 * E * A * F
+
+F32 = mybir.dt.float32
+BF16 = mybir.dt.bfloat16
+I32 = mybir.dt.int32
+U32 = mybir.dt.uint32
+U8 = mybir.dt.uint8
+FP8 = mybir.dt.float8_e4m3fn
+FP8X4 = mybir.dt.float8_e4m3fn_x4
+FP4X4 = mybir.dt.float4_e2m1fn_x4
+MULT = mybir.AluOpType.mult
+ADD = mybir.AluOpType.add
+COPY = mybir.ActivationFunctionType.Copy
+
+P = 128
+T = 4
+S = L // (P * T)
+G = E // (P * T)
+FT = F // P
+
+TILES = [(0, 512), (512, 512), (1024, 512)]
+CHUNKS = [(0, 0, 256), (0, 256, 256), (1, 0, 512), (2, 0, 512)]
+
+
+def tile_robust_information_block_s13_kernel(tc, d, basis_bytes, basis_scale, r, ja_words, ja_scales, out):
+    nc = tc.nc
+    with ExitStack() as ctx:
+        keep = ctx.enter_context(tc.tile_pool(name="keep", bufs=1))
+        planes = ctx.enter_context(tc.tile_pool(name="planes", bufs=3))
+        stage = ctx.enter_context(tc.tile_pool(name="stage", bufs=4))
+        psum = ctx.enter_context(tc.psum_pool(name="psum", bufs=1))
+        ctx.enter_context(tc.manual_schedule())
+
+        ident = keep.tile([P, P], F32, name="ident")
+        make_identity(nc, ident[:])
+        warm = keep.tile([P, 1], F32, name="warm")
+        nc.vector.memset(warm[:], 1.0)
+        js = keep.tile([P, G * F], U8, name="js", align_bytes=64)
+        nc.gpsimd.memset(js[:].bitcast(I32), 0)
+
+        bscale = keep.tile([P, S, T], F32, name="bscale")
+        nc.scalar.dma_start(out=bscale[:], in_=basis_scale.rearrange("(s p t) o -> p s (t o)", p=P, t=T))
+        rt = keep.tile([P, G, T], BF16, name="rt")
+        nc.scalar.dma_start(out=rt[:], in_=r.rearrange("(g p t) -> p g t", p=P, t=T))
+        warm2 = keep.tile([P, 1], F32, name="warm2")
+        nc.scalar.activation(out=warm2[:], in_=warm[:], func=COPY)
+
+        bview = basis_bytes.rearrange("(s p t) n -> s p t n", p=P, t=T)
+        braw = []
+        for c0, width in [(0, 512), (512, 1024)]:
+            braw.append([keep.tile([P, T, width], U8, name="braw_%d_%d" % (c0, s)) for s in range(S)])
+        dview = d.rearrange("(g p t) k -> g p t k", p=P, t=T)
+        draw = [keep.tile([P, T, L], BF16, name="draw_%d" % g) for g in range(G)]
+
+        def load_basis(h):
+            c0, width = [(0, 512), (512, 1024)][h]
+            for s in range(S):
+                nc.sync.dma_start(out=braw[h][s][:], in_=bview[s][:, :, c0 : c0 + width])
+
+        def load_d(g, n):
+            for t in range(0, T, n):
+                nc.sync.dma_start(out=draw[g][:, t : t + n, :], in_=dview[g][:, t : t + n, :])
+
+        load_basis(0)
+        load_d(0, 1)
+        load_d(1, 2)
+        load_basis(1)
+        load_d(2, 2)
+        load_d(3, 2)
+        jw = keep.tile([P, G, 2 * F], U8, name="jw", align_bytes=64)
+        nc.sync.dma_start(out=jw[:], in_=ja_words.rearrange("g p n -> p g n"))
+        for q in range(4):
+            nc.sync.dma_start(
+                out=js[32 * q : 32 * q + 4, :].rearrange("p (g n) -> p g n", g=G).bitcast(I32),
+                in_=ja_scales[:, 4 * q : 4 * q + 4, :].rearrange("g q n -> q g n").bitcast(I32),
+            )
+
+        bq = [keep.tile([P, S * w], U32, name="bq_%d" % c0, align_bytes=64) for c0, w in TILES]
+        bs = [keep.tile([P, S * w], U8, name="bs_%d" % c0, align_bytes=64) for c0, w in TILES]
+        dq = [keep.tile([P, T * S * P], U32, name="dq_%d" % g, align_bytes=64) for g in range(G)]
+        ds = [keep.tile([P, T * S * P], U8, name="ds_%d" % g, align_bytes=64) for g in range(G)]
+        wq = [[keep.tile([P, w], U32, name="wq_%d_%d" % (c0, g), align_bytes=64) for g in range(G)] for c0, w in TILES]
+        ws = [[keep.tile([P, w], U8, name="ws_%d_%d" % (c0, g), align_bytes=64) for g in range(G)] for c0, w in TILES]
+
+        weight = keep.tile([P, G * T], F32, name="weight")
+
+        def weights():
+            rr = rt[:].rearrange("p g t -> p (g t)")
+            sq = keep.tile([P, G * T], F32, name="sq")
+            nc.vector.tensor_tensor(out=sq[:], in0=rr, in1=rr, op=MULT)
+            den = keep.tile([P, G * T], F32, name="den")
+            nc.vector.tensor_scalar(out=den[:], in0=sq[:], scalar1=1.0, scalar2=None, op0=ADD)
+            nc.vector.reciprocal(out=weight[:], in_=den[:])
+
+        wide = {}
+        grouped = {}
+
+        def widen(i, s, t, eng):
+            j, o, w = CHUNKS[i]
+            if (i, s) not in wide:
+                wide[i, s] = planes.tile([P, T, 512], BF16, name="wide", align_bytes=64)
+            h = 0 if j == 0 else 1
+            o += 512 * (j - h)
+            src = braw[h][s][:, t, o : o + w].bitcast(FP8)
+            dst = wide[i, s][:, t, :w]
+            if eng == "v":
+                nc.vector.tensor_scalar(out=dst, in0=src, scalar1=bscale[:, s, t : t + 1], scalar2=None, op0=MULT)
+            else:
+                nc.scalar.activation(out=dst, in_=src, func=COPY, scale=bscale[:, s, t : t + 1])
+
+        def interleave(i, s, eng):
+            w = CHUNKS[i][2]
+            grouped[i, s] = planes.tile([P, 512, T], BF16, name="grouped", align_bytes=64)
+            src = wide[i, s][:, :, :w].rearrange("p t n -> p n t")
+            dst = grouped[i, s][:, :w, :]
+            if eng == "v":
+                nc.vector.tensor_copy(out=dst, in_=src)
+            else:
+                nc.scalar.copy(out=dst, in_=src)
+
+        def quant_basis(i, s):
+            j, o, w = CHUNKS[i]
+            o += s * TILES[j][1]
+            nc.vector.quantize_mx(
+                out=bq[j][:, o : o + w].bitcast(FP8X4),
+                scales=bs[j][:, o : o + w],
+                in_=grouped[i, s][:, :w, :].rearrange("p n t -> p (n t)"),
+            )
+
+        tbank = {}
+        dgrp = {}
+
+        def transpose(g, t):
+            b = 4 + t
+            bank = psum.tile([P, 512], F32, name="bank_%d" % b)
+            tbank[g, t] = bank
+            words = draw[g][:, t, :].bitcast(F32)
+            for s in range(S):
+                for u in range(2):
+                    o = (2 * s + u) * P
+                    nc.tensor.transpose(bank[:, o : o + P], words[:, 256 * s + u : 256 * (s + 1) : 2], ident[:])
+
+        def copy_d(g, t, eng="s"):
+            dg = stage.tile([P, S * P * T], BF16, name="dg", align_bytes=64)
+            dgrp[g, t] = dg
+            dst = dg[:].bitcast(F32).rearrange("p (s e u) -> p s e u", s=S, u=2)
+            src = tbank[g, t][:].rearrange("p (s u e) -> p s e u", s=S, u=2)
+            if eng == "s":
+                nc.scalar.copy(out=dst, in_=src)
+            else:
+                nc.vector.tensor_copy(out=dst, in_=src)
+
+        def quant_d(g, t):
+            o = t * S * P
+            nc.vector.quantize_mx(
+                out=dq[g][:, o : o + S * P].bitcast(FP8X4), scales=ds[g][:, o : o + S * P], in_=dgrp[g, t][:]
+            )
+
+        jbank = {}
+        wj = {}
+        wplane = {}
+        units = []
+
+        def product(bank, o, n, j, g, t, c):
+            w = TILES[j][1]
+            for s in range(S):
+                m = (t * S + s) * P
+                nc.tensor.matmul_mx(
+                    out=bank[:, o : o + n],
+                    lhsT=dq[g][:, m : m + P].bitcast(FP8X4),
+                    lhsT_scale=ds[g][:, m : m + P],
+                    rhs=bq[j][:, s * w + c : s * w + c + n].bitcast(FP8X4),
+                    rhs_scale=bs[j][:, s * w + c : s * w + c + n],
+                    start=(s == 0),
+                    stop=(s == S - 1),
+                )
+
+        def stage1(u):
+            path, j, g, b = units[u]
+            bank = psum.tile([P, 512], F32, name="bank_%d" % (u % 4))
+            jbank[u] = bank
+            if path == "A":
+                for t in range(T):
+                    product(bank, t * P, P, j, g, t, b * P)
+            else:
+                product(bank, 0, TILES[j][1], j, g, b, 0)
+
+        def evacuate(u):
+            path, j, g, b = units[u]
+            if path == "A":
+                if (j, g) not in wj:
+                    wj[j, g] = stage.tile([P, 512, T], BF16, name="wj", align_bytes=64)
+                nc.vector.tensor_tensor(
+                    out=wj[j, g][:, b * P : (b + 1) * P, :],
+                    in0=jbank[u][:].rearrange("p (t n) -> p n t", t=T),
+                    in1=weight[:, g * T : (g + 1) * T].unsqueeze(1).to_broadcast([P, P, T]),
+                    op=MULT,
+                )
+            else:
+                if (j, g) not in wplane:
+                    wplane[j, g] = stage.tile([P, T, 512], BF16, name="wplane", align_bytes=64)
+                nc.scalar.activation(
+                    out=wplane[j, g][:, b, :], in_=jbank[u][:], func=COPY, scale=weight[:, g * T + b : g * T + b + 1]
+                )
+
+        def interleave_wj(j, g):
+            wj[j, g] = stage.tile([P, 512, T], BF16, name="wj", align_bytes=64)
+            nc.vector.tensor_copy(out=wj[j, g][:], in_=wplane[j, g][:].rearrange("p t n -> p n t"))
+
+        def quant_wj(j, g, c=0, n=512):
+            nc.vector.quantize_mx(
+                out=wq[j][g][:, c : c + n].bitcast(FP8X4),
+                scales=ws[j][g][:, c : c + n],
+                in_=wj[j, g][:, c : c + n, :].rearrange("p n t -> p (n t)"),
+            )
+
+        hbank = {}
+
+        def stage2(j, f, gs, first=0, last=G - 1):
+            w = TILES[j][1]
+            if gs[0] == 0:
+                hbank[j, f] = psum.tile([P, 512], F32, name="bank_%d" % (0 if j == 1 and f == 3 else 4 + f))
+            for g in gs:
+                nc.tensor.matmul_mx(
+                    out=hbank[j, f][:, :w],
+                    lhsT=jw[:, g, 2 * P * f : 2 * P * (f + 1)].bitcast(FP4X4),
+                    lhsT_scale=js[:, g * F + f * P : g * F + (f + 1) * P],
+                    rhs=wq[j][g][:].bitcast(FP8X4),
+                    rhs_scale=ws[j][g][:],
+                    start=(g == first),
+                    stop=(g == last),
+                )
+
+        def store(j, f, eng="s"):
+            c0, w = TILES[j]
+            h = stage.tile([P, 512], F32, name="h")
+            if eng == "s":
+                nc.scalar.copy(out=h[:, :w], in_=hbank[j, f][:, :w])
+            else:
+                nc.vector.tensor_copy(out=h[:, :w], in_=hbank[j, f][:, :w])
+            nc.sync.dma_start(out=out[f * P : (f + 1) * P, c0 : c0 + w], in_=h[:, :w])
+
+        for t in range(3):
+            widen(0, 0, t, "v")
+        widen(0, 0, 3, "s")
+        for t in range(2):
+            widen(0, 1, t, "v")
+        for t in range(2, T):
+            widen(0, 1, t, "s")
+        interleave(0, 0, "v")
+        weights()
+        interleave(0, 1, "v")
+        for t in range(T):
+            transpose(0, t)
+        for t in range(T):
+            widen(1, 0, t, "s")
+        quant_basis(0, 0)
+        copy_d(0, 0)
+        quant_basis(0, 1)
+        widen(1, 1, 0, "s")
+        widen(1, 1, 1, "s")
+        interleave(1, 0, "v")
+        copy_d(0, 1)
+        quant_d(0, 0)
+        widen(1, 1, 2, "s")
+        widen(1, 1, 3, "s")
+        quant_d(0, 1)
+        copy_d(0, 2)
+        quant_basis(1, 0)
+        copy_d(0, 3)
+        interleave(1, 1, "v")
+        quant_d(0, 2)
+        for t in range(T):
+            transpose(1, t)
+        quant_d(0, 3)
+        quant_basis(1, 1)
+        for t in range(T):
+            copy_d(1, t)
+
+        for j in range(3):
+            for g in range(0, G, 2):
+                order = "AAAAAAAA" if j == 0 else "ABABABAB"
+                if j == 2 and g == 2:
+                    order = "BBBABAAA"
+                n = [0, 0]
+                for i, p in enumerate(order):
+                    k = int(p == "B" or (j == 0 and i > 3))
+                    units.append((p, j, g + k, n[k]))
+                    n[k] += 1
+        extra = {}
+
+        def at(u, f, *args):
+            extra.setdefault(u, []).append((f, args))
+
+        for t in range(T):
+            at(1 + t // 2, quant_d, 1, t)
+        for g in (2, 3):
+            for t in range(T):
+                u = 4 * g - 4 + 2 * (t // 2)
+                at(u, transpose, g, t)
+                at(u, copy_d, g, t)
+                at(u + 1, quant_d, g, t)
+        for t in range(T):
+            at(1 + t // 2, widen, 2, 0, t, "s")
+            at(5 + 2 * (t // 2), widen, 2, 1, t, "s")
+            at(12 + t, widen, 3, 0, t, "s")
+            at(16 + t, widen, 3, 1, t, "s")
+        at(5, interleave, 2, 0, "v")
+        at(8, quant_basis, 2, 0)
+        at(11, interleave, 2, 1, "s")
+        at(14, quant_basis, 2, 1)
+        at(20, interleave, 3, 0, "v")
+        at(22, quant_basis, 3, 0)
+        at(26, interleave, 3, 1, "v")
+        at(28, quant_basis, 3, 1)
+        for g in range(G):
+            at(4 * g + 6, quant_wj, 0, g)
+        for j in (1, 2):
+            for g in range(G):
+                u = 16 * j + 8 * (g // 2 + 1)
+                if u < 48:
+                    if g % 2:
+                        at(u + 2, interleave_wj, j, g)
+                        at(u + 3, quant_wj, j, g)
+                    else:
+                        at(u + 1, quant_wj, j, g)
+        for f in range(FT):
+            at(20 + 3 * f, stage2, 0, f, range(G))
+            at(21 + 3 * f, store, 0, f)
+            at(36 + f if f < 3 else 48, stage2, 1, f, range(G))
+            at(37 + f if f < 3 else 48, store, 1, f)
+        at(46, interleave_wj, 2, 3)
+        at(47, quant_wj, 2, 3)
+        for f in range(FT):
+            at(44, stage2, 2, f, [0])
+            at(46, stage2, 2, f, [1])
+            at(49, stage2, 2, f, [3], 0, 2)
+        n = len(units)
+        for u in range(n + 2):
+            for f, args in extra.get(u, []):
+                f(*args)
+            if u < n:
+                stage1(u)
+            if 0 < u <= n:
+                evacuate(u - 1)
+        quant_wj(2, 2)
+        for f in range(FT):
+            stage2(2, f, [2], last=2)
+            store(2, f, "sv"[f % 2])

@@ -22,334 +22,344 @@ P = 128
 T = 4
 S = L // (P * T)
 G = E // (P * T)
-FT = F // P
+W = 512
+J = A // W
+R = F // P
+STEPS = J * G * T
 
-TILES = [(0, 512), (512, 512), (1024, 512)]
-CHUNKS = [(0, 0, 256), (0, 256, 256), (1, 0, 512), (2, 0, 512)]
+PIECES = [(0, 0, 256), (0, 256, 256), (1, 0, 512), (2, 0, 512)]
+
+ROUNDS = [(0, g, "0000") for g in range(G)] + [(j, g, "01010101") for j in (1, 2) for g in (0, 2)]
+ROUNDS[-1] = (2, 2, "11101000")
 
 
 def tile_robust_information_block_s13_kernel(tc, d, basis_bytes, basis_scale, r, ja_words, ja_scales, out):
     nc = tc.nc
     with ExitStack() as ctx:
         keep = ctx.enter_context(tc.tile_pool(name="keep", bufs=1))
-        planes = ctx.enter_context(tc.tile_pool(name="planes", bufs=3))
+        convert = ctx.enter_context(tc.tile_pool(name="convert", bufs=3))
         stage = ctx.enter_context(tc.tile_pool(name="stage", bufs=4))
         psum = ctx.enter_context(tc.psum_pool(name="psum", bufs=1))
         ctx.enter_context(tc.manual_schedule())
 
+        def bank(k):
+            return psum.tile([P, W], F32, name="bank_%d" % k)
+
         ident = keep.tile([P, P], F32, name="ident")
         make_identity(nc, ident[:])
-        warm = keep.tile([P, 1], F32, name="warm")
-        nc.vector.memset(warm[:], 1.0)
-        js = keep.tile([P, G * F], U8, name="js", align_bytes=64)
-        nc.gpsimd.memset(js[:].bitcast(I32), 0)
+        zeros = keep.tile([P, W], BF16, name="zeros")
+        nc.vector.memset(zeros[:], 0.0)
+        ja_scale = keep.tile([P, G * F], U8, name="ja_scale", align_bytes=64)
+        nc.gpsimd.memset(ja_scale[:].bitcast(I32), 0)
 
-        bscale = keep.tile([P, S, T], F32, name="bscale")
-        nc.scalar.dma_start(out=bscale[:], in_=basis_scale.rearrange("(s p t) o -> p s (t o)", p=P, t=T))
-        rt = keep.tile([P, G, T], BF16, name="rt")
-        nc.scalar.dma_start(out=rt[:], in_=r.rearrange("(g p t) -> p g t", p=P, t=T))
-        warm2 = keep.tile([P, 1], F32, name="warm2")
-        nc.scalar.activation(out=warm2[:], in_=warm[:], func=COPY)
+        row_scale = keep.tile([P, S, T], F32, name="row_scale")
+        nc.scalar.dma_start(out=row_scale[:], in_=basis_scale.rearrange("(s p t) o -> p s (t o)", p=P, t=T))
+        table = keep.tile([P, 1], F32, name="table")
+        nc.scalar.activation(out=table[:], in_=zeros[:, 0:1], func=COPY)
 
-        bview = basis_bytes.rearrange("(s p t) n -> s p t n", p=P, t=T)
-        braw = []
-        for c0, width in [(0, 512), (512, 1024)]:
-            braw.append([keep.tile([P, T, width], U8, name="braw_%d_%d" % (c0, s)) for s in range(S)])
-        dview = d.rearrange("(g p t) k -> g p t k", p=P, t=T)
-        draw = [keep.tile([P, T, L], BF16, name="draw_%d" % g) for g in range(G)]
+        code_rows = basis_bytes.rearrange("(s p t) n -> s p t n", p=P, t=T)
+        codes_first = [keep.tile([P, T, W], U8, name="codes_first_%d" % s) for s in range(S)]
+        codes_rest = [keep.tile([P, T, A - W], U8, name="codes_rest_%d" % s) for s in range(S)]
+        d_rows = d.rearrange("(g p t) k -> g p t k", p=P, t=T)
+        d_raw = [keep.tile([P, T, L], BF16, name="d_raw_%d" % g) for g in range(G)]
 
-        def load_basis(h):
-            c0, width = [(0, 512), (512, 1024)][h]
-            for s in range(S):
-                nc.sync.dma_start(out=braw[h][s][:], in_=bview[s][:, :, c0 : c0 + width])
+        def load_d(g, t, n):
+            nc.sync.dma_start(out=d_raw[g][:, t : t + n, :], in_=d_rows[g][:, t : t + n, :])
 
-        def load_d(g, n):
-            for t in range(0, T, n):
-                nc.sync.dma_start(out=draw[g][:, t : t + n, :], in_=dview[g][:, t : t + n, :])
-
-        load_basis(0)
-        load_d(0, 1)
-        load_d(1, 2)
-        load_basis(1)
-        load_d(2, 2)
-        load_d(3, 2)
-        jw = keep.tile([P, G, 2 * F], U8, name="jw", align_bytes=64)
-        nc.sync.dma_start(out=jw[:], in_=ja_words.rearrange("g p n -> p g n"))
+        for s in range(S):
+            nc.sync.dma_start(out=codes_first[s][:], in_=code_rows[s][:, :, :W])
+            load_d(0, 2 * s, 1)
+            if s == 0:
+                load_d(0, 1, 1)
+        load_d(0, 3, 1)
+        load_d(1, 0, 2)
+        load_d(1, 2, 2)
+        residual = keep.tile([P, G, T], BF16, name="residual")
+        nc.sync.dma_start(out=residual[:], in_=r.rearrange("(g p t) -> p g t", p=P, t=T))
+        for s in range(S):
+            nc.sync.dma_start(out=codes_rest[s][:], in_=code_rows[s][:, :, W:])
+        for g in (2, 3):
+            load_d(g, 0, 2)
+            load_d(g, 2, 2)
+        ja = keep.tile([P, G, 2 * F], U8, name="ja", align_bytes=64)
+        nc.sync.dma_start(out=ja[:], in_=ja_words.rearrange("g p n -> p g n"))
         for q in range(4):
             nc.sync.dma_start(
-                out=js[32 * q : 32 * q + 4, :].rearrange("p (g n) -> p g n", g=G).bitcast(I32),
+                out=ja_scale[32 * q : 32 * q + 4, :].rearrange("p (g n) -> p g n", g=G).bitcast(I32),
                 in_=ja_scales[:, 4 * q : 4 * q + 4, :].rearrange("g q n -> q g n").bitcast(I32),
             )
 
-        bq = [keep.tile([P, S * w], U32, name="bq_%d" % c0, align_bytes=64) for c0, w in TILES]
-        bs = [keep.tile([P, S * w], U8, name="bs_%d" % c0, align_bytes=64) for c0, w in TILES]
-        dq = [keep.tile([P, T * S * P], U32, name="dq_%d" % g, align_bytes=64) for g in range(G)]
-        ds = [keep.tile([P, T * S * P], U8, name="ds_%d" % g, align_bytes=64) for g in range(G)]
-        wq = [[keep.tile([P, w], U32, name="wq_%d_%d" % (c0, g), align_bytes=64) for g in range(G)] for c0, w in TILES]
-        ws = [[keep.tile([P, w], U8, name="ws_%d_%d" % (c0, g), align_bytes=64) for g in range(G)] for c0, w in TILES]
+        basis_q = [keep.tile([P, S * W], U32, name="basis_q_%d" % j, align_bytes=64) for j in range(J)]
+        basis_s = [keep.tile([P, S * W], U8, name="basis_s_%d" % j, align_bytes=64) for j in range(J)]
+        d_q = [keep.tile([P, T * S * P], U32, name="d_q_%d" % g, align_bytes=64) for g in range(G)]
+        d_s = [keep.tile([P, T * S * P], U8, name="d_s_%d" % g, align_bytes=64) for g in range(G)]
+        wj_q = [[keep.tile([P, W], U32, name="wj_q_%d_%d" % (j, g), align_bytes=64) for g in range(G)] for j in range(J)]
+        wj_s = [[keep.tile([P, W], U8, name="wj_s_%d_%d" % (j, g), align_bytes=64) for g in range(G)] for j in range(J)]
+
+        def copy_on(engine, dst, src):
+            if engine == "vector":
+                nc.vector.tensor_copy(out=dst, in_=src)
+            else:
+                nc.scalar.copy(out=dst, in_=src)
+
+        def interleave_on(engine, dst, src):
+            copy_on(
+                engine,
+                dst.rearrange("p (c i) t -> p c t i", i=4),
+                src.rearrange("p t (c i) -> p c t i", i=4),
+            )
 
         weight = keep.tile([P, G * T], F32, name="weight")
 
-        def weights():
-            rr = rt[:].rearrange("p g t -> p (g t)")
-            sq = keep.tile([P, G * T], F32, name="sq")
-            nc.vector.tensor_tensor(out=sq[:], in0=rr, in1=rr, op=MULT)
-            den = keep.tile([P, G * T], F32, name="den")
-            nc.vector.tensor_scalar(out=den[:], in0=sq[:], scalar1=1.0, scalar2=None, op0=ADD)
-            nc.vector.reciprocal(out=weight[:], in_=den[:])
+        def make_weights():
+            values = residual[:].rearrange("p g t -> p (g t)")
+            square = keep.tile([P, G * T], F32, name="square")
+            nc.vector.tensor_tensor(out=square[:], in0=values, in1=values, op=MULT)
+            denominator = keep.tile([P, G * T], F32, name="denominator")
+            nc.vector.tensor_scalar(out=denominator[:], in0=square[:], scalar1=1.0, scalar2=None, op0=ADD)
+            nc.vector.reciprocal(out=weight[:], in_=denominator[:])
 
-        wide = {}
-        grouped = {}
+        plane = {}
+        interleaved = {}
 
-        def widen(i, s, t, eng):
-            j, o, w = CHUNKS[i]
-            if (i, s) not in wide:
-                wide[i, s] = planes.tile([P, T, 512], BF16, name="wide", align_bytes=64)
-            h = 0 if j == 0 else 1
-            o += 512 * (j - h)
-            src = braw[h][s][:, t, o : o + w].bitcast(FP8)
-            dst = wide[i, s][:, t, :w]
-            if eng == "v":
-                nc.vector.tensor_scalar(out=dst, in0=src, scalar1=bscale[:, s, t : t + 1], scalar2=None, op0=MULT)
+        def widen(i, s, t, engine):
+            j, c, n = PIECES[i]
+            if (i, s) not in plane:
+                plane[i, s] = convert.tile([P, T, W], BF16, name="plane", align_bytes=64)
+            if j == 0:
+                codes = codes_first[s][:, t, c : c + n]
             else:
-                nc.scalar.activation(out=dst, in_=src, func=COPY, scale=bscale[:, s, t : t + 1])
-
-        def interleave(i, s, eng):
-            w = CHUNKS[i][2]
-            grouped[i, s] = planes.tile([P, 512, T], BF16, name="grouped", align_bytes=64)
-            src = wide[i, s][:, :, :w].rearrange("p t n -> p n t")
-            dst = grouped[i, s][:, :w, :]
-            if eng == "v":
-                nc.vector.tensor_copy(out=dst, in_=src)
+                codes = codes_rest[s][:, t, W * (j - 1) : W * j]
+            dst = plane[i, s][:, t, :n]
+            scale = row_scale[:, s, t : t + 1]
+            if engine == "vector":
+                nc.vector.tensor_scalar(out=dst, in0=codes.bitcast(FP8), scalar1=scale, scalar2=None, op0=MULT)
             else:
-                nc.scalar.copy(out=dst, in_=src)
+                nc.scalar.activation(out=dst, in_=codes.bitcast(FP8), func=COPY, scale=scale)
 
-        def quant_basis(i, s):
-            j, o, w = CHUNKS[i]
-            o += s * TILES[j][1]
+        def interleave_basis(i, s, engine):
+            n = PIECES[i][2]
+            interleaved[i, s] = convert.tile([P, W, T], BF16, name="interleaved", align_bytes=64)
+            interleave_on(engine, interleaved[i, s][:, :n, :], plane[i, s][:, :, :n])
+
+        def quantize_basis(i, s):
+            j, c, n = PIECES[i]
+            c += s * W
             nc.vector.quantize_mx(
-                out=bq[j][:, o : o + w].bitcast(FP8X4),
-                scales=bs[j][:, o : o + w],
-                in_=grouped[i, s][:, :w, :].rearrange("p n t -> p (n t)"),
+                out=basis_q[j][:, c : c + n].bitcast(FP8X4),
+                scales=basis_s[j][:, c : c + n],
+                in_=interleaved[i, s][:, :n, :].rearrange("p n t -> p (n t)"),
             )
 
-        tbank = {}
-        dgrp = {}
+        sorted_d = {}
+        d_bank = {}
+        d_grouped = {}
 
-        def transpose(g, t):
-            b = 4 + t
-            bank = psum.tile([P, 512], F32, name="bank_%d" % b)
-            tbank[g, t] = bank
-            words = draw[g][:, t, :].bitcast(F32)
+        def sort_words(g, t):
+            sorted_d[g, t] = stage.tile([P, L], BF16, name="sorted_d")
+            nc.vector.tensor_copy(
+                out=sorted_d[g, t][:].bitcast(F32).rearrange("p (s u q) -> p s u q", s=S, u=2),
+                in_=d_raw[g][:, t, :].bitcast(F32).rearrange("p (s q u) -> p s u q", s=S, u=2),
+            )
+
+        def transpose_d(g, t):
+            d_bank[g, t] = bank(4 + t)
             for s in range(S):
                 for u in range(2):
                     o = (2 * s + u) * P
-                    nc.tensor.transpose(bank[:, o : o + P], words[:, 256 * s + u : 256 * (s + 1) : 2], ident[:])
+                    if (g, t) in sorted_d:
+                        words = sorted_d[g, t][:].bitcast(F32)[:, o : o + P]
+                    else:
+                        words = d_raw[g][:, t, :].bitcast(F32)[:, 2 * P * s + u : 2 * P * (s + 1) : 2]
+                    nc.tensor.transpose(d_bank[g, t][:, o : o + P], words, ident[:])
 
-        def copy_d(g, t, eng="s"):
-            dg = stage.tile([P, S * P * T], BF16, name="dg", align_bytes=64)
-            dgrp[g, t] = dg
-            dst = dg[:].bitcast(F32).rearrange("p (s e u) -> p s e u", s=S, u=2)
-            src = tbank[g, t][:].rearrange("p (s u e) -> p s e u", s=S, u=2)
-            if eng == "s":
-                nc.scalar.copy(out=dst, in_=src)
-            else:
-                nc.vector.tensor_copy(out=dst, in_=src)
-
-        def quant_d(g, t):
-            o = t * S * P
-            nc.vector.quantize_mx(
-                out=dq[g][:, o : o + S * P].bitcast(FP8X4), scales=ds[g][:, o : o + S * P], in_=dgrp[g, t][:]
+        def copy_d(g, t):
+            d_grouped[g, t] = stage.tile([P, S * P * T], BF16, name="d_grouped", align_bytes=64)
+            nc.scalar.copy(
+                out=d_grouped[g, t][:].bitcast(F32).rearrange("p (s e u) -> p s e u", s=S, u=2),
+                in_=d_bank[g, t][:].rearrange("p (s u e) -> p s e u", s=S, u=2),
             )
 
-        jbank = {}
-        wj = {}
-        wplane = {}
-        units = []
+        def quantize_d(g, t):
+            columns = slice(t * S * P, (t + 1) * S * P)
+            nc.vector.quantize_mx(
+                out=d_q[g][:, columns].bitcast(FP8X4), scales=d_s[g][:, columns], in_=d_grouped[g, t][:]
+            )
 
-        def product(bank, o, n, j, g, t, c):
-            w = TILES[j][1]
+        by_vector = [(0, 0), (0, 1), (0, 2)]
+        steps = []
+        for j, g0, turns in ROUNDS:
+            for i, turn in enumerate(turns):
+                steps.append((j, g0 + int(turn), turns[:i].count(turn)))
+        jb_bank = {}
+        wj_plane = {}
+        wj = {}
+
+        def product(dst, j, g, t, c, n):
             for s in range(S):
-                m = (t * S + s) * P
+                stationary = slice((t * S + s) * P, (t * S + s + 1) * P)
+                moving = slice(s * W + c, s * W + c + n)
                 nc.tensor.matmul_mx(
-                    out=bank[:, o : o + n],
-                    lhsT=dq[g][:, m : m + P].bitcast(FP8X4),
-                    lhsT_scale=ds[g][:, m : m + P],
-                    rhs=bq[j][:, s * w + c : s * w + c + n].bitcast(FP8X4),
-                    rhs_scale=bs[j][:, s * w + c : s * w + c + n],
+                    out=dst,
+                    lhsT=d_q[g][:, stationary].bitcast(FP8X4),
+                    lhsT_scale=d_s[g][:, stationary],
+                    rhs=basis_q[j][:, moving].bitcast(FP8X4),
+                    rhs_scale=basis_s[j][:, moving],
                     start=(s == 0),
                     stop=(s == S - 1),
                 )
 
-        def stage1(u):
-            path, j, g, b = units[u]
-            bank = psum.tile([P, 512], F32, name="bank_%d" % (u % 4))
-            jbank[u] = bank
-            if path == "A":
+        def stage_1(step):
+            j, g, b = steps[step]
+            jb_bank[step] = bank(step % 4)
+            if (j, g) in by_vector:
                 for t in range(T):
-                    product(bank, t * P, P, j, g, t, b * P)
+                    product(jb_bank[step][:, t * P : (t + 1) * P], j, g, t, b * P, P)
             else:
-                product(bank, 0, TILES[j][1], j, g, b, 0)
+                product(jb_bank[step][:], j, g, b, 0, W)
 
-        def evacuate(u):
-            path, j, g, b = units[u]
-            if path == "A":
-                if (j, g) not in wj:
-                    wj[j, g] = stage.tile([P, 512, T], BF16, name="wj", align_bytes=64)
+        def empty(step):
+            j, g, b = steps[step]
+            if (j, g) in by_vector:
+                if b == 0:
+                    wj[j, g] = stage.tile([P, W, T], BF16, name="wj", align_bytes=64)
                 nc.vector.tensor_tensor(
                     out=wj[j, g][:, b * P : (b + 1) * P, :],
-                    in0=jbank[u][:].rearrange("p (t n) -> p n t", t=T),
+                    in0=jb_bank[step][:].rearrange("p (t n) -> p n t", t=T),
                     in1=weight[:, g * T : (g + 1) * T].unsqueeze(1).to_broadcast([P, P, T]),
                     op=MULT,
                 )
             else:
-                if (j, g) not in wplane:
-                    wplane[j, g] = stage.tile([P, T, 512], BF16, name="wplane", align_bytes=64)
+                if b == 0:
+                    wj_plane[j, g] = stage.tile([P, T, W], BF16, name="wj_plane", align_bytes=64)
                 nc.scalar.activation(
-                    out=wplane[j, g][:, b, :], in_=jbank[u][:], func=COPY, scale=weight[:, g * T + b : g * T + b + 1]
+                    out=wj_plane[j, g][:, b, :],
+                    in_=jb_bank[step][:],
+                    func=COPY,
+                    scale=weight[:, g * T + b : g * T + b + 1],
                 )
 
         def interleave_wj(j, g):
-            wj[j, g] = stage.tile([P, 512, T], BF16, name="wj", align_bytes=64)
-            nc.vector.tensor_copy(out=wj[j, g][:], in_=wplane[j, g][:].rearrange("p t n -> p n t"))
+            wj[j, g] = stage.tile([P, W, T], BF16, name="wj", align_bytes=64)
+            interleave_on("vector", wj[j, g][:], wj_plane[j, g][:])
 
-        def quant_wj(j, g, c=0, n=512):
+        def quantize_wj(j, g):
             nc.vector.quantize_mx(
-                out=wq[j][g][:, c : c + n].bitcast(FP8X4),
-                scales=ws[j][g][:, c : c + n],
-                in_=wj[j, g][:, c : c + n, :].rearrange("p n t -> p (n t)"),
+                out=wj_q[j][g][:].bitcast(FP8X4),
+                scales=wj_s[j][g][:],
+                in_=wj[j, g][:].rearrange("p n t -> p (n t)"),
             )
 
-        hbank = {}
+        h_bank = {}
 
-        def stage2(j, f, gs, first=0, last=G - 1):
-            w = TILES[j][1]
-            if gs[0] == 0:
-                hbank[j, f] = psum.tile([P, 512], F32, name="bank_%d" % (0 if j == 1 and f == 3 else 4 + f))
-            for g in gs:
+        def stage_2(j, f):
+            h_bank[j, f] = bank(f if j == J - 1 else 4 + f)
+            for g in range(G):
                 nc.tensor.matmul_mx(
-                    out=hbank[j, f][:, :w],
-                    lhsT=jw[:, g, 2 * P * f : 2 * P * (f + 1)].bitcast(FP4X4),
-                    lhsT_scale=js[:, g * F + f * P : g * F + (f + 1) * P],
-                    rhs=wq[j][g][:].bitcast(FP8X4),
-                    rhs_scale=ws[j][g][:],
-                    start=(g == first),
-                    stop=(g == last),
+                    out=h_bank[j, f][:],
+                    lhsT=ja[:, g, 2 * P * f : 2 * P * (f + 1)].bitcast(FP4X4),
+                    lhsT_scale=ja_scale[:, g * F + f * P : g * F + (f + 1) * P],
+                    rhs=wj_q[j][g][:].bitcast(FP8X4),
+                    rhs_scale=wj_s[j][g][:],
+                    start=(g == 0),
+                    stop=(g == G - 1),
                 )
 
-        def store(j, f, eng="s"):
-            c0, w = TILES[j]
-            h = stage.tile([P, 512], F32, name="h")
-            if eng == "s":
-                nc.scalar.copy(out=h[:, :w], in_=hbank[j, f][:, :w])
-            else:
-                nc.vector.tensor_copy(out=h[:, :w], in_=hbank[j, f][:, :w])
-            nc.sync.dma_start(out=out[f * P : (f + 1) * P, c0 : c0 + w], in_=h[:, :w])
+        def store(j, f, parts):
+            h = stage.tile([P, W], F32, name="h")
+            for engine, c, n in parts:
+                copy_on(engine, h[:, c : c + n], h_bank[j, f][:, c : c + n])
+            for engine, c, n in parts:
+                nc.sync.dma_start(out=out[f * P : (f + 1) * P, j * W + c : j * W + c + n], in_=h[:, c : c + n])
 
+        def keep_clock(n):
+            for k in range(n):
+                nc.tensor.matmul(out=bank(k % 4)[:], lhsT=zeros[:, :P], rhs=zeros[:], start=True, stop=True)
+
+        keep_clock(6)
         for t in range(3):
-            widen(0, 0, t, "v")
-        widen(0, 0, 3, "s")
-        for t in range(2):
-            widen(0, 1, t, "v")
-        for t in range(2, T):
-            widen(0, 1, t, "s")
-        interleave(0, 0, "v")
-        weights()
-        interleave(0, 1, "v")
+            widen(0, 0, t, "vector")
+        widen(0, 0, 3, "scalar")
         for t in range(T):
-            transpose(0, t)
+            widen(0, 1, t, "vector" if t < 2 else "scalar")
+        for s in range(S):
+            interleave_basis(0, s, "vector")
+        for t in range(0, T, 2):
+            transpose_d(0, t)
+            transpose_d(0, t + 1)
+            keep_clock(2)
+        for s in range(S):
+            quantize_basis(0, s)
         for t in range(T):
-            widen(1, 0, t, "s")
-        quant_basis(0, 0)
-        copy_d(0, 0)
-        quant_basis(0, 1)
-        widen(1, 1, 0, "s")
-        widen(1, 1, 1, "s")
-        interleave(1, 0, "v")
-        copy_d(0, 1)
-        quant_d(0, 0)
-        widen(1, 1, 2, "s")
-        widen(1, 1, 3, "s")
-        quant_d(0, 1)
-        copy_d(0, 2)
-        quant_basis(1, 0)
-        copy_d(0, 3)
-        interleave(1, 1, "v")
-        quant_d(0, 2)
+            copy_d(0, t)
         for t in range(T):
-            transpose(1, t)
-        quant_d(0, 3)
-        quant_basis(1, 1)
-        for t in range(T):
-            copy_d(1, t)
+            widen(1, t // 2, 2 * (t % 2), "vector")
+            widen(1, t // 2, 2 * (t % 2) + 1, "vector")
+            quantize_d(0, t)
+        make_weights()
+        for s in range(S):
+            interleave_basis(1, s, "vector")
 
-        for j in range(3):
-            for g in range(0, G, 2):
-                order = "AAAAAAAA" if j == 0 else "ABABABAB"
-                if j == 2 and g == 2:
-                    order = "BBBABAAA"
-                n = [0, 0]
-                for i, p in enumerate(order):
-                    k = int(p == "B" or (j == 0 and i > 3))
-                    units.append((p, j, g + k, n[k]))
-                    n[k] += 1
-        extra = {}
+        work = {}
 
-        def at(u, f, *args):
-            extra.setdefault(u, []).append((f, args))
+        def before(step, job, *args):
+            work.setdefault(step, []).append((job, args))
 
-        for t in range(T):
-            at(1 + t // 2, quant_d, 1, t)
-        for g in (2, 3):
+        for s in range(S):
+            before(1, quantize_basis, 1, s)
+        for g in range(1, G):
             for t in range(T):
-                u = 4 * g - 4 + 2 * (t // 2)
-                at(u, transpose, g, t)
-                at(u, copy_d, g, t)
-                at(u + 1, quant_d, g, t)
+                run = max(0, 4 * g - 5 + 2 * (t // 2))
+                if g == 3 and t >= 2:
+                    before(run - 3, sort_words, g, t)
+                before(run, transpose_d, g, t)
+                before(run, copy_d, g, t)
+                before(run + 1, quantize_d, g, t)
         for t in range(T):
-            at(1 + t // 2, widen, 2, 0, t, "s")
-            at(5 + 2 * (t // 2), widen, 2, 1, t, "s")
-            at(12 + t, widen, 3, 0, t, "s")
-            at(16 + t, widen, 3, 1, t, "s")
-        at(5, interleave, 2, 0, "v")
-        at(8, quant_basis, 2, 0)
-        at(11, interleave, 2, 1, "s")
-        at(14, quant_basis, 2, 1)
-        at(20, interleave, 3, 0, "v")
-        at(22, quant_basis, 3, 0)
-        at(26, interleave, 3, 1, "v")
-        at(28, quant_basis, 3, 1)
+            before(t, widen, 2, 0, t, "scalar")
+            before(3 + t, widen, 2, 1, t, "scalar")
+            before(7 + 2 * t, widen, 3, 0, t, "scalar" if t < 2 else "vector")
+            before(16 + 2 * t, widen, 3, 1, t, "vector")
+        before(5, interleave_basis, 2, 0, "vector")
+        before(8, quantize_basis, 2, 0)
+        before(10, interleave_basis, 2, 1, "scalar")
+        before(13, quantize_basis, 2, 1)
+        for s in range(S):
+            before(23, interleave_basis, 3, s, "vector")
+            before(32, quantize_basis, 3, s)
+        before(21, interleave_wj, 0, 3)
         for g in range(G):
-            at(4 * g + 6, quant_wj, 0, g)
+            before(4 * g + 18, quantize_wj, 0, g)
         for j in (1, 2):
             for g in range(G):
-                u = 16 * j + 8 * (g // 2 + 1)
-                if u < 48:
-                    if g % 2:
-                        at(u + 2, interleave_wj, j, g)
-                        at(u + 3, quant_wj, j, g)
-                    else:
-                        at(u + 1, quant_wj, j, g)
-        for f in range(FT):
-            at(20 + 3 * f, stage2, 0, f, range(G))
-            at(21 + 3 * f, store, 0, f)
-            at(36 + f if f < 3 else 48, stage2, 1, f, range(G))
-            at(37 + f if f < 3 else 48, store, 1, f)
-        at(46, interleave_wj, 2, 3)
-        at(47, quant_wj, 2, 3)
-        for f in range(FT):
-            at(44, stage2, 2, f, [0])
-            at(46, stage2, 2, f, [1])
-            at(49, stage2, 2, f, [3], 0, 2)
-        n = len(units)
-        for u in range(n + 2):
-            for f, args in extra.get(u, []):
-                f(*args)
-            if u < n:
-                stage1(u)
-            if 0 < u <= n:
-                evacuate(u - 1)
-        quant_wj(2, 2)
-        for f in range(FT):
-            stage2(2, f, [2], last=2)
-            store(2, f, "sv"[f % 2])
+                end = 16 * j + 8 * (g // 2 + 1)
+                if end < STEPS:
+                    before(end + 5 + g % 2, interleave_wj, j, g)
+                    before(end + 6 + g % 2, quantize_wj, j, g)
+        before(46, interleave_wj, 2, 3)
+        before(47, quantize_wj, 2, 3)
+        for f in range(R):
+            before(31, stage_2, 0, f)
+            before(32, store, 0, f, [("vector", 0, W)])
+        before(45, stage_2, 1, 0)
+        before(46, store, 1, 0, [("vector", 0, W)])
+
+        for step in range(STEPS):
+            for job, args in work.get(step, []):
+                job(*args)
+            stage_1(step)
+            if step > 0:
+                empty(step - 1)
+        empty(STEPS - 1)
+
+        interleave_wj(2, 2)
+        quantize_wj(2, 2)
+        for f in range(1, R):
+            stage_2(1, f)
+            store(1, f, [("vector", 0, W)])
+        for f in range(R):
+            stage_2(2, f)
+            if f < R - 1:
+                store(2, f, [("vector" if f % 2 else "scalar", 0, W)])
+            else:
+                store(2, f, [("vector", W // 2, W // 2), ("scalar", 0, W // 2)])

from contextlib import ExitStack

import concourse.mybir as mybir
from concourse.masks import make_identity

E, L, A, F = 2048, 1024, 1536, 512
FLOPS = 2 * E * L * A + 2 * E * A * F

F32 = mybir.dt.float32
BF16 = mybir.dt.bfloat16
I32 = mybir.dt.int32
U32 = mybir.dt.uint32
U8 = mybir.dt.uint8
FP8 = mybir.dt.float8_e4m3fn
FP8X4 = mybir.dt.float8_e4m3fn_x4
FP4X4 = mybir.dt.float4_e2m1fn_x4
MULT = mybir.AluOpType.mult
ADD = mybir.AluOpType.add
COPY = mybir.ActivationFunctionType.Copy

P = 128
T = 4
S = L // (P * T)
G = E // (P * T)
W = 512
J = A // W
R = F // P
STEPS = J * G * T

PIECES = [(0, 0, 256), (0, 256, 256), (1, 0, 512), (2, 0, 512)]

ROUNDS = [(0, g, "0000") for g in range(G)] + [(j, g, "01010101") for j in (1, 2) for g in (0, 2)]
ROUNDS[-1] = (2, 2, "11101000")


def tile_robust_information_block_s13_kernel(tc, d, basis_bytes, basis_scale, r, ja_words, ja_scales, out):
    nc = tc.nc
    with ExitStack() as ctx:
        keep = ctx.enter_context(tc.tile_pool(name="keep", bufs=1))
        convert = ctx.enter_context(tc.tile_pool(name="convert", bufs=3))
        stage = ctx.enter_context(tc.tile_pool(name="stage", bufs=4))
        psum = ctx.enter_context(tc.psum_pool(name="psum", bufs=1))
        ctx.enter_context(tc.manual_schedule())

        def bank(k):
            return psum.tile([P, W], F32, name="bank_%d" % k)

        ident = keep.tile([P, P], F32, name="ident")
        make_identity(nc, ident[:])
        zeros = keep.tile([P, W], BF16, name="zeros")
        nc.vector.memset(zeros[:], 0.0)
        ja_scale = keep.tile([P, G * F], U8, name="ja_scale", align_bytes=64)
        nc.gpsimd.memset(ja_scale[:].bitcast(I32), 0)

        row_scale = keep.tile([P, S, T], F32, name="row_scale")
        nc.scalar.dma_start(out=row_scale[:], in_=basis_scale.rearrange("(s p t) o -> p s (t o)", p=P, t=T))
        table = keep.tile([P, 1], F32, name="table")
        nc.scalar.activation(out=table[:], in_=zeros[:, 0:1], func=COPY)

        code_rows = basis_bytes.rearrange("(s p t) n -> s p t n", p=P, t=T)
        codes_first = [keep.tile([P, T, W], U8, name="codes_first_%d" % s) for s in range(S)]
        codes_rest = [keep.tile([P, T, A - W], U8, name="codes_rest_%d" % s) for s in range(S)]
        d_rows = d.rearrange("(g p t) k -> g p t k", p=P, t=T)
        d_raw = [keep.tile([P, T, L], BF16, name="d_raw_%d" % g) for g in range(G)]

        def load_d(g, t, n):
            nc.sync.dma_start(out=d_raw[g][:, t : t + n, :], in_=d_rows[g][:, t : t + n, :])

        for s in range(S):
            nc.sync.dma_start(out=codes_first[s][:], in_=code_rows[s][:, :, :W])
            load_d(0, 2 * s, 1)
            if s == 0:
                load_d(0, 1, 1)
        load_d(0, 3, 1)
        load_d(1, 0, 2)
        load_d(1, 2, 2)
        residual = keep.tile([P, G, T], BF16, name="residual")
        nc.sync.dma_start(out=residual[:], in_=r.rearrange("(g p t) -> p g t", p=P, t=T))
        for s in range(S):
            nc.sync.dma_start(out=codes_rest[s][:], in_=code_rows[s][:, :, W:])
        for g in (2, 3):
            load_d(g, 0, 2)
            load_d(g, 2, 2)
        ja = keep.tile([P, G, 2 * F], U8, name="ja", align_bytes=64)
        nc.sync.dma_start(out=ja[:], in_=ja_words.rearrange("g p n -> p g n"))
        for q in range(4):
            nc.sync.dma_start(
                out=ja_scale[32 * q : 32 * q + 4, :].rearrange("p (g n) -> p g n", g=G).bitcast(I32),
                in_=ja_scales[:, 4 * q : 4 * q + 4, :].rearrange("g q n -> q g n").bitcast(I32),
            )

        basis_q = [keep.tile([P, S * W], U32, name="basis_q_%d" % j, align_bytes=64) for j in range(J)]
        basis_s = [keep.tile([P, S * W], U8, name="basis_s_%d" % j, align_bytes=64) for j in range(J)]
        d_q = [keep.tile([P, T * S * P], U32, name="d_q_%d" % g, align_bytes=64) for g in range(G)]
        d_s = [keep.tile([P, T * S * P], U8, name="d_s_%d" % g, align_bytes=64) for g in range(G)]
        wj_q = [[keep.tile([P, W], U32, name="wj_q_%d_%d" % (j, g), align_bytes=64) for g in range(G)] for j in range(J)]
        wj_s = [[keep.tile([P, W], U8, name="wj_s_%d_%d" % (j, g), align_bytes=64) for g in range(G)] for j in range(J)]

        def copy_on(engine, dst, src):
            if engine == "vector":
                nc.vector.tensor_copy(out=dst, in_=src)
            else:
                nc.scalar.copy(out=dst, in_=src)

        def interleave_on(engine, dst, src):
            copy_on(
                engine,
                dst.rearrange("p (c i) t -> p c t i", i=4),
                src.rearrange("p t (c i) -> p c t i", i=4),
            )

        weight = keep.tile([P, G * T], F32, name="weight")

        def make_weights():
            values = residual[:].rearrange("p g t -> p (g t)")
            square = keep.tile([P, G * T], F32, name="square")
            nc.vector.tensor_tensor(out=square[:], in0=values, in1=values, op=MULT)
            denominator = keep.tile([P, G * T], F32, name="denominator")
            nc.vector.tensor_scalar(out=denominator[:], in0=square[:], scalar1=1.0, scalar2=None, op0=ADD)
            nc.vector.reciprocal(out=weight[:], in_=denominator[:])

        plane = {}
        interleaved = {}

        def widen(i, s, t, engine):
            j, c, n = PIECES[i]
            if (i, s) not in plane:
                plane[i, s] = convert.tile([P, T, W], BF16, name="plane", align_bytes=64)
            if j == 0:
                codes = codes_first[s][:, t, c : c + n]
            else:
                codes = codes_rest[s][:, t, W * (j - 1) : W * j]
            dst = plane[i, s][:, t, :n]
            scale = row_scale[:, s, t : t + 1]
            if engine == "vector":
                nc.vector.tensor_scalar(out=dst, in0=codes.bitcast(FP8), scalar1=scale, scalar2=None, op0=MULT)
            else:
                nc.scalar.activation(out=dst, in_=codes.bitcast(FP8), func=COPY, scale=scale)

        def interleave_basis(i, s, engine):
            n = PIECES[i][2]
            interleaved[i, s] = convert.tile([P, W, T], BF16, name="interleaved", align_bytes=64)
            interleave_on(engine, interleaved[i, s][:, :n, :], plane[i, s][:, :, :n])

        def quantize_basis(i, s):
            j, c, n = PIECES[i]
            c += s * W
            nc.vector.quantize_mx(
                out=basis_q[j][:, c : c + n].bitcast(FP8X4),
                scales=basis_s[j][:, c : c + n],
                in_=interleaved[i, s][:, :n, :].rearrange("p n t -> p (n t)"),
            )

        sorted_d = {}
        d_bank = {}
        d_grouped = {}

        def sort_words(g, t):
            sorted_d[g, t] = stage.tile([P, L], BF16, name="sorted_d")
            nc.vector.tensor_copy(
                out=sorted_d[g, t][:].bitcast(F32).rearrange("p (s u q) -> p s u q", s=S, u=2),
                in_=d_raw[g][:, t, :].bitcast(F32).rearrange("p (s q u) -> p s u q", s=S, u=2),
            )

        def transpose_d(g, t):
            d_bank[g, t] = bank(4 + t)
            for s in range(S):
                for u in range(2):
                    o = (2 * s + u) * P
                    if (g, t) in sorted_d:
                        words = sorted_d[g, t][:].bitcast(F32)[:, o : o + P]
                    else:
                        words = d_raw[g][:, t, :].bitcast(F32)[:, 2 * P * s + u : 2 * P * (s + 1) : 2]
                    nc.tensor.transpose(d_bank[g, t][:, o : o + P], words, ident[:])

        def copy_d(g, t):
            d_grouped[g, t] = stage.tile([P, S * P * T], BF16, name="d_grouped", align_bytes=64)
            nc.scalar.copy(
                out=d_grouped[g, t][:].bitcast(F32).rearrange("p (s e u) -> p s e u", s=S, u=2),
                in_=d_bank[g, t][:].rearrange("p (s u e) -> p s e u", s=S, u=2),
            )

        def quantize_d(g, t):
            columns = slice(t * S * P, (t + 1) * S * P)
            nc.vector.quantize_mx(
                out=d_q[g][:, columns].bitcast(FP8X4), scales=d_s[g][:, columns], in_=d_grouped[g, t][:]
            )

        by_vector = [(0, 0), (0, 1), (0, 2)]
        steps = []
        for j, g0, turns in ROUNDS:
            for i, turn in enumerate(turns):
                steps.append((j, g0 + int(turn), turns[:i].count(turn)))
        jb_bank = {}
        wj_plane = {}
        wj = {}

        def product(dst, j, g, t, c, n):
            for s in range(S):
                stationary = slice((t * S + s) * P, (t * S + s + 1) * P)
                moving = slice(s * W + c, s * W + c + n)
                nc.tensor.matmul_mx(
                    out=dst,
                    lhsT=d_q[g][:, stationary].bitcast(FP8X4),
                    lhsT_scale=d_s[g][:, stationary],
                    rhs=basis_q[j][:, moving].bitcast(FP8X4),
                    rhs_scale=basis_s[j][:, moving],
                    start=(s == 0),
                    stop=(s == S - 1),
                )

        def stage_1(step):
            j, g, b = steps[step]
            jb_bank[step] = bank(step % 4)
            if (j, g) in by_vector:
                for t in range(T):
                    product(jb_bank[step][:, t * P : (t + 1) * P], j, g, t, b * P, P)
            else:
                product(jb_bank[step][:], j, g, b, 0, W)

        def empty(step):
            j, g, b = steps[step]
            if (j, g) in by_vector:
                if b == 0:
                    wj[j, g] = stage.tile([P, W, T], BF16, name="wj", align_bytes=64)
                nc.vector.tensor_tensor(
                    out=wj[j, g][:, b * P : (b + 1) * P, :],
                    in0=jb_bank[step][:].rearrange("p (t n) -> p n t", t=T),
                    in1=weight[:, g * T : (g + 1) * T].unsqueeze(1).to_broadcast([P, P, T]),
                    op=MULT,
                )
            else:
                if b == 0:
                    wj_plane[j, g] = stage.tile([P, T, W], BF16, name="wj_plane", align_bytes=64)
                nc.scalar.activation(
                    out=wj_plane[j, g][:, b, :],
                    in_=jb_bank[step][:],
                    func=COPY,
                    scale=weight[:, g * T + b : g * T + b + 1],
                )

        def interleave_wj(j, g):
            wj[j, g] = stage.tile([P, W, T], BF16, name="wj", align_bytes=64)
            interleave_on("vector", wj[j, g][:], wj_plane[j, g][:])

        def quantize_wj(j, g):
            nc.vector.quantize_mx(
                out=wj_q[j][g][:].bitcast(FP8X4),
                scales=wj_s[j][g][:],
                in_=wj[j, g][:].rearrange("p n t -> p (n t)"),
            )

        h_bank = {}

        def stage_2(j, f):
            h_bank[j, f] = bank(f if j == J - 1 else 4 + f)
            for g in range(G):
                nc.tensor.matmul_mx(
                    out=h_bank[j, f][:],
                    lhsT=ja[:, g, 2 * P * f : 2 * P * (f + 1)].bitcast(FP4X4),
                    lhsT_scale=ja_scale[:, g * F + f * P : g * F + (f + 1) * P],
                    rhs=wj_q[j][g][:].bitcast(FP8X4),
                    rhs_scale=wj_s[j][g][:],
                    start=(g == 0),
                    stop=(g == G - 1),
                )

        def store(j, f, parts):
            h = stage.tile([P, W], F32, name="h")
            for engine, c, n in parts:
                copy_on(engine, h[:, c : c + n], h_bank[j, f][:, c : c + n])
            for engine, c, n in parts:
                nc.sync.dma_start(out=out[f * P : (f + 1) * P, j * W + c : j * W + c + n], in_=h[:, c : c + n])

        def keep_clock(n):
            for k in range(n):
                nc.tensor.matmul(out=bank(k % 4)[:], lhsT=zeros[:, :P], rhs=zeros[:], start=True, stop=True)

        keep_clock(6)
        for t in range(3):
            widen(0, 0, t, "vector")
        widen(0, 0, 3, "scalar")
        for t in range(T):
            widen(0, 1, t, "vector" if t < 2 else "scalar")
        for s in range(S):
            interleave_basis(0, s, "vector")
        for t in range(0, T, 2):
            transpose_d(0, t)
            transpose_d(0, t + 1)
            keep_clock(2)
        for s in range(S):
            quantize_basis(0, s)
        for t in range(T):
            copy_d(0, t)
        for t in range(T):
            widen(1, t // 2, 2 * (t % 2), "vector")
            widen(1, t // 2, 2 * (t % 2) + 1, "vector")
            quantize_d(0, t)
        make_weights()
        for s in range(S):
            interleave_basis(1, s, "vector")

        work = {}

        def before(step, job, *args):
            work.setdefault(step, []).append((job, args))

        for s in range(S):
            before(1, quantize_basis, 1, s)
        for g in range(1, G):
            for t in range(T):
                run = max(0, 4 * g - 5 + 2 * (t // 2))
                if g == 3 and t >= 2:
                    before(run - 3, sort_words, g, t)
                before(run, transpose_d, g, t)
                before(run, copy_d, g, t)
                before(run + 1, quantize_d, g, t)
        for t in range(T):
            before(t, widen, 2, 0, t, "scalar")
            before(3 + t, widen, 2, 1, t, "scalar")
            before(7 + 2 * t, widen, 3, 0, t, "scalar" if t < 2 else "vector")
            before(16 + 2 * t, widen, 3, 1, t, "vector")
        before(5, interleave_basis, 2, 0, "vector")
        before(8, quantize_basis, 2, 0)
        before(10, interleave_basis, 2, 1, "scalar")
        before(13, quantize_basis, 2, 1)
        for s in range(S):
            before(23, interleave_basis, 3, s, "vector")
            before(32, quantize_basis, 3, s)
        before(21, interleave_wj, 0, 3)
        for g in range(G):
            before(4 * g + 18, quantize_wj, 0, g)
        for j in (1, 2):
            for g in range(G):
                end = 16 * j + 8 * (g // 2 + 1)
                if end < STEPS:
                    before(end + 5 + g % 2, interleave_wj, j, g)
                    before(end + 6 + g % 2, quantize_wj, j, g)
        before(46, interleave_wj, 2, 3)
        before(47, quantize_wj, 2, 3)
        for f in range(R):
            before(31, stage_2, 0, f)
            before(32, store, 0, f, [("vector", 0, W)])
        before(45, stage_2, 1, 0)
        before(46, store, 1, 0, [("vector", 0, W)])

        for step in range(STEPS):
            for job, args in work.get(step, []):
                job(*args)
            stage_1(step)
            if step > 0:
                empty(step - 1)
        empty(STEPS - 1)

        interleave_wj(2, 2)
        quantize_wj(2, 2)
        for f in range(1, R):
            stage_2(1, f)
            store(1, f, [("vector", 0, W)])
        for f in range(R):
            stage_2(2, f)
            if f < R - 1:
                store(2, f, [("vector" if f % 2 else "scalar", 0, W)])
            else:
                store(2, f, [("vector", W // 2, W // 2), ("scalar", 0, W // 2)])
